import numpy as np
import ml_dtypes


def mxq(x, axis, fmt="e4m3"):
    dtype, down = {"e4m3": (ml_dtypes.float8_e4m3fn, 7), "e5m2": (ml_dtypes.float8_e5m2, 14)}[fmt]
    v = np.moveaxis(np.asarray(x, np.float32).astype(ml_dtypes.bfloat16).astype(np.float64), axis, -1)
    blocks = v.reshape(v.shape[:-1] + (-1, 32))
    amax = np.abs(blocks).max(-1, keepdims=True)
    byte = np.maximum(np.where(amax > 0, np.frexp(amax)[1] - 1 + 127, 0) - down, 1)
    scale = np.exp2(byte - 127.0)
    codes = (blocks / scale).astype(np.float32).astype(dtype).astype(np.float64)
    return np.moveaxis((codes * scale).reshape(v.shape), -1, axis)


WIDE = False


def mx_kscale(k):
    if not WIDE:
        return np.ones(k)
    levels = np.array([30, -30])
    if k % 512:
        return np.exp2(np.random.permutation(np.resize(levels, k // 32))).repeat(32)
    a = np.empty((k // 512, 16))
    for p in range(k // 512):
        a[p, :8] = np.random.permutation(np.resize(levels, 8))
        for g in range(8):
            far = levels[np.abs(levels - a[p, g]) >= 10]
            a[p, g + 8] = far[np.random.randint(len(far))]
    return np.exp2(a.ravel()).repeat(32)


def f64(x):
    return np.asarray(x).astype(np.float64)


def striped(idx):
    return np.tile(np.asarray(idx).reshape(-1, 16).T, (8, 1)).astype(np.uint16)


def unstriped(offs):
    return offs[:16].T.reshape(-1).astype(np.int64)


E2M1 = np.array([0.0, 0.5, 1.0, 1.5, 2.0, 3.0, 4.0, 6.0, -0.0, -0.5, -1.0, -1.5, -2.0, -3.0, -4.0, -6.0])


def pack_weight(w, fmt):
    k, n = w.shape
    w = f64(np.asarray(w, np.float32).astype(ml_dtypes.bfloat16)).reshape(k // 32, 32, n)
    amax = np.abs(w).max(1)
    if fmt == "e4m3":
        byte = np.frexp(amax)[1] - 1 + 127 - 7
    else:
        mant, ex = np.frexp(amax / 6.0)
        byte = np.where(mant > 0.5, ex, ex - 1) + 127
    byte = np.clip(np.where(amax > 0, byte, 1), 1, 254)
    scaled = (w * np.exp2(127.0 - byte)[:, None, :]).reshape(k, n).astype(np.float32)
    by_word = np.ascontiguousarray(scaled.reshape(k // 512, 128, 4, n).transpose(0, 1, 3, 2))
    if fmt == "e4m3":
        words = by_word.astype(ml_dtypes.float8_e4m3fn).view(np.uint8)
    else:
        c = by_word.astype(ml_dtypes.float4_e2m1fn).view(np.uint8) & 0xF
        words = (c[..., 0::2] | (c[..., 1::2] << 4)).reshape(k // 512, 128, 2 * n)
    return np.ascontiguousarray(words), np.ascontiguousarray(byte.astype(np.uint8).reshape(k // 512, 16, n))


def unpack_weight(words, scales, fmt):
    g, _, n = scales.shape
    words = np.ascontiguousarray(words).reshape(g, 128, n, -1)
    if fmt == "e4m3":
        vals = words.view(ml_dtypes.float8_e4m3fn).astype(np.float64)
    else:
        nib = np.empty((g, 128, n, 4), np.uint8)
        nib[..., 0::2] = words & 0xF
        nib[..., 1::2] = words >> 4
        vals = E2M1[nib]
    vals = vals * np.repeat(np.exp2(scales.astype(np.float64) - 127.0), 8, axis=1)[..., None]
    return vals.transpose(0, 1, 3, 2).reshape(g * 512, n)


K, T, Z, J, R, C, O, N, E = 512, 1024, 1024, 256, 512, 512, 256, 256, 1024


def setup_inputs():
    n = np.random.standard_normal
    idx = np.random.permutation(T)[:J]
    idx2 = np.random.permutation(Z)[:J]
    idx3 = np.random.permutation(C)[:J]
    idx4 = np.random.permutation(C)[:J]
    idx5 = np.random.permutation(C)[:O]
    idx6 = np.random.permutation(C)[:O]
    idx7 = np.random.permutation(E)[:O]
    fk = mx_kscale(K)
    fr = mx_kscale(R)
    xtp = pack_weight(n((K, T)) / fk[:, None], "e2m1")
    xop = pack_weight(n((K, Z)) / fk[:, None], "e4m3")
    wp = pack_weight(n((K, R)) * 1 / np.sqrt(K) * fk[:, None] * fr, "e4m3")
    wbp = pack_weight(n((R, N)) * 1 / np.sqrt(R) / fr[:, None], "e2m1")
    return {
        "xt_words": xtp[0],
        "xt_scales": xtp[1],
        "xo_words": xop[0],
        "xo_scales": xop[1],
        "w_words": wp[0],
        "w_scales": wp[1],
        "wb_words": wbp[0],
        "wb_scales": wbp[1],
        "tz": (n((N, E))).astype(np.float32),
        "offs": striped(idx),
        "offs2": striped(idx2),
        "offs3": striped(idx3),
        "offs4": striped(idx4),
        "offs5": striped(idx5),
        "offs6": striped(idx6),
        "offs7": striped(idx7),
    }


def reference(xt_words, xt_scales, xo_words, xo_scales, w_words, w_scales, wb_words, wb_scales, tz, offs, offs2, offs3, offs4, offs5, offs6, offs7):
    idx = unstriped(offs)
    idx2 = unstriped(offs2)
    idx3 = unstriped(offs3)
    idx4 = unstriped(offs4)
    idx5 = unstriped(offs5)
    idx6 = unstriped(offs6)
    idx7 = unstriped(offs7)
    xtu = unpack_weight(xt_words, xt_scales, "e2m1")
    xou = unpack_weight(xo_words, xo_scales, "e4m3")
    wu = unpack_weight(w_words, w_scales, "e4m3")
    wbu = unpack_weight(wb_words, wb_scales, "e2m1")
    xtidxg = xtu[:, idx]
    a = wu.T @ xtidxg
    xoidx2g = xou[:, idx2]
    b = wu.T @ xoidx2g
    pw = np.zeros((R, C))
    pw[:, idx3] = a
    pv = np.zeros((R, C))
    pv[:, idx4] = b
    hid = np.abs(pw[:, idx5] - pv[:, idx6])
    hidq = mxq(hid, 0, "e5m2")
    p = wbu.T @ hidq
    y = p + f64(tz)[:, idx7]
    return y

@@ -1,0 +1,187 @@
+from contextlib import ExitStack
+
+import concourse.mybir as mybir
+
+K, T, Z, J, R, C, O, N, E = 512, 1024, 1024, 256, 512, 512, 256, 256, 1024
+FLOPS = 2 * K * R * J * 2 + 2 * R * N * O
+
+F32 = mybir.dt.float32
+BF16 = mybir.dt.bfloat16
+I32 = mybir.dt.int32
+U32 = mybir.dt.uint32
+U16 = mybir.dt.uint16
+U8 = mybir.dt.uint8
+E4M3X4 = mybir.dt.float8_e4m3fn_x4
+E5M2X4 = mybir.dt.float8_e5m2_x4
+E2M1X4 = mybir.dt.float4_e2m1fn_x4
+ACT = mybir.ActivationFunctionType
+ALU = mybir.AluOpType
+
+P = 128
+PACK = 4
+
+
+def tile_list_oneforboth_twoboards_one_tabled_kernel(
+    tc, xt_words, xt_scales, xo_words, xo_scales, w_words, w_scales, wb_words, wb_scales, tz,
+    offs, offs2, offs3, offs4, offs5, offs6, offs7, out,
+):
+    nc = tc.nc
+    with ExitStack() as ctx:
+        keep = ctx.enter_context(tc.tile_pool(name="keep", bufs=1))
+        psum = ctx.enter_context(tc.psum_pool(name="psum", bufs=1))
+
+        def load_list(name, src):
+            tile = keep.tile([P, src.shape[1]], U16, name=name)
+            nc.sync.dma_start(tile[:], src)
+            return tile
+
+        def scale_plane(name, width, engine):
+            tile = keep.tile([P, width], U8, name=name, align_bytes=64)
+            return tile
+
+        def load_scales(tile, src, queue):
+            for q in range(4):
+                queue.dma_start(
+                    tile[32 * q : 32 * q + 32, :].bitcast(I32),
+                    src[0, 4 * q : 4 * q + 4, :].bitcast(I32).partition_broadcast(8),
+                )
+
+        xt_s = scale_plane("xt_s", T, nc.vector)
+        w_s = scale_plane("w_s", R, nc.vector)
+        xo_s = scale_plane("xo_s", Z, nc.vector)
+        wb_s = scale_plane("wb_s", N, nc.vector)
+
+        l_xt = load_list("l_xt", offs)
+        xt_w = keep.tile([P, T], U16, align_bytes=64)
+        nc.sync.dma_start(xt_w[:].bitcast(I32), xt_words[0].bitcast(I32))
+        w_w = keep.tile([P, R], I32, align_bytes=64)
+        nc.scalar.dma_start(w_w[:], w_words[0].rearrange("p n t -> p (n t)").bitcast(I32))
+        load_scales(xt_s, xt_scales, nc.sync)
+        load_scales(w_s, w_scales, nc.scalar)
+        l_pw_put = load_list("l_pw_put", offs3)
+        l_xo = load_list("l_xo", offs2)
+        xo_w = keep.tile([P, Z], U32, align_bytes=64)
+        nc.sync.dma_start(xo_w[:].bitcast(I32), xo_words[0].rearrange("p n t -> p (n t)").bitcast(I32))
+        load_scales(xo_s, xo_scales, nc.sync)
+        l_pv_put = load_list("l_pv_put", offs4)
+        l_pw_get = load_list("l_pw_get", offs5)
+        l_pv_get = load_list("l_pv_get", offs6)
+        l_tz = load_list("l_tz", offs7)
+        tz_sb = [keep.tile([P, E], F32, name="tz%d" % h) for h in range(2)]
+        for h in range(2):
+            nc.sync.dma_start(tz_sb[h][:], tz[h * P : (h + 1) * P, :])
+        wb_w = keep.tile([P, 2 * N], U8, align_bytes=64)
+        nc.sync.dma_start(wb_w[:].bitcast(I32), wb_words[0].bitcast(I32))
+        load_scales(wb_s, wb_scales, nc.sync)
+
+        pw = [keep.tile([P, C], F32, name="pw%d" % t) for t in range(PACK)]
+        pv = [keep.tile([P, C], F32, name="pv%d" % t) for t in range(PACK)]
+        for board in pw + pv:
+            nc.vector.memset(board[:], 0.0)
+
+        xt_gw = keep.tile([P, J], U16, align_bytes=64)
+        xt_gs = keep.tile([P, J], U8, align_bytes=64)
+        nc.vector.tensor_copy(xt_gw[:], xt_w[:].indirect(l_xt[:]))
+        nc.vector.tensor_copy(xt_gs[:], xt_s[:].indirect(l_xt[:]))
+
+        wp_w = keep.tile([P, R], I32, align_bytes=64)
+        wp_s = keep.tile([P, R], U8, align_bytes=64)
+        nc.vector.tensor_copy(
+            wp_w[:].rearrange("p (t c i) -> p c t i", t=PACK, i=4),
+            w_w[:].rearrange("p (c i t) -> p c t i", t=PACK, i=4),
+        )
+        nc.vector.tensor_copy(
+            wp_s[:].rearrange("p (t c i) -> p c t i", t=PACK, i=16),
+            w_s[:].rearrange("p (c i t) -> p c t i", t=PACK, i=16),
+        )
+
+        def first_stage(name, codes, scales):
+            banks = [psum.tile([P, 2, J], F32, name="%s_ps%d" % (name, u)) for u in range(2)]
+            for t in range(PACK):
+                cols = slice(t * P, (t + 1) * P)
+                nc.tensor.matmul_mx(
+                    out=banks[t // 2][:, t % 2, :],
+                    lhsT=wp_w[:, cols].bitcast(E4M3X4), lhsT_scale=wp_s[:, cols],
+                    rhs=codes, rhs_scale=scales, start=True, stop=True,
+                )
+            return banks
+
+        a_ps = first_stage("a", xt_gw[:].bitcast(E2M1X4), xt_gs[:])
+        a_sb = [keep.tile([P, 2, J], F32, name="a_sb%d" % u) for u in range(2)]
+        b_sb = [keep.tile([P, 2, J], F32, name="b_sb%d" % u) for u in range(2)]
+
+        def put(engine, board, lst, src):
+            if engine == "v":
+                nc.vector.tensor_copy(board[:].indirect(lst[:]), src)
+            else:
+                nc.scalar.activation(board[:].indirect(lst[:]), src, ACT.Copy)
+
+        def get(engine, dst, window, lst):
+            if engine == "v":
+                nc.vector.tensor_copy(dst, window[:].indirect(lst[:]))
+            else:
+                nc.scalar.activation(dst, window[:].indirect(lst[:]), ACT.Copy)
+
+        nc.scalar.copy(a_sb[0][:], a_ps[0][:])
+        put("s", pw[0], l_pw_put, a_sb[0][:, 0, :])
+        put("v", pw[1], l_pw_put, a_sb[0][:, 1, :])
+        nc.scalar.copy(a_sb[1][:], a_ps[1][:])
+        put("s", pw[2], l_pw_put, a_sb[1][:, 0, :])
+        put("s", pw[3], l_pw_put, a_sb[1][:, 1, :])
+
+        xo_gw = keep.tile([P, J], U32, align_bytes=64)
+        xo_gs = keep.tile([P, J], U8, align_bytes=64)
+        nc.vector.tensor_copy(xo_gw[:], xo_w[:].indirect(l_xo[:]))
+        nc.vector.tensor_copy(xo_gs[:], xo_s[:].indirect(l_xo[:]))
+        b_ps = first_stage("b", xo_gw[:].bitcast(E4M3X4), xo_gs[:])
+
+        nc.scalar.copy(b_sb[0][:], b_ps[0][:])
+        put("v", pv[0], l_pv_put, b_sb[0][:, 0, :])
+        put("v", pv[1], l_pv_put, b_sb[0][:, 1, :])
+        nc.scalar.copy(b_sb[1][:], b_ps[1][:])
+        put("s", pv[2], l_pv_put, b_sb[1][:, 0, :])
+        put("s", pv[3], l_pv_put, b_sb[1][:, 1, :])
+
+        pw_g = [keep.tile([P, O], F32, name="pw_g%d" % t) for t in range(PACK)]
+        diff = keep.tile([P, PACK, O], F32)
+        tz_g = keep.tile([P, 2, O], F32)
+        for t in range(PACK):
+            get("v", pw_g[t][:], pw[t], l_pw_get)
+        for t in range(PACK - 1):
+            nc.vector.tensor_tensor(diff[:, t, :], pv[t][:].indirect(l_pv_get[:]), pw_g[t][:], ALU.subtract)
+        get("s", tz_g[:, 0, :], tz_sb[0], l_tz)
+        HALF = O // 2
+        hid = keep.tile([P, O, PACK], BF16, align_bytes=64)
+        hid_w = keep.tile([P, O], U32, align_bytes=64)
+        hid_s = keep.tile([P, O], U8, align_bytes=64)
+        t = PACK - 1
+        for u in range(2):
+            cols = slice(u * HALF, (u + 1) * HALF)
+            nc.vector.tensor_tensor(
+                diff[:, t, cols], pv[t][:].indirect(l_pv_get[:, u * 8 : (u + 1) * 8]), pw_g[t][:, cols], ALU.subtract
+            )
+        get("v", tz_g[:, 1, :], tz_sb[1], l_tz)
+        for u in range(2):
+            cols = slice(u * HALF, (u + 1) * HALF)
+            nc.scalar.activation(
+                hid[:, cols, :].rearrange("p (c i) t -> p c t i", i=4),
+                diff[:, :, cols].rearrange("p t (c i) -> p c t i", i=4),
+                ACT.Abs,
+            )
+        for u in range(2):
+            cols = slice(u * HALF, (u + 1) * HALF)
+            nc.vector.quantize_mx(
+                out=hid_w[:, cols].bitcast(E5M2X4), scales=hid_s[:, cols],
+                in_=hid[:, cols, :].rearrange("p o t -> p (o t)"),
+            )
+            p_ps = psum.tile([P, 2, HALF], F32, name="p_ps%d" % u)
+            y = keep.tile([P, 2, HALF], F32, name="y%d" % u)
+            for h in range(2):
+                nc.tensor.matmul_mx(
+                    out=p_ps[:, h, :],
+                    lhsT=wb_w[:, 2 * P * h : 2 * P * (h + 1)].bitcast(E2M1X4), lhsT_scale=wb_s[:, P * h : P * (h + 1)],
+                    rhs=hid_w[:, cols].bitcast(E5M2X4), rhs_scale=hid_s[:, cols], start=True, stop=True,
+                )
+            nc.vector.tensor_tensor(y[:], p_ps[:], tz_g[:, :, cols], ALU.add)
+            queue = nc.sync if u == 0 else nc.scalar
+            queue.dma_start(out[:, cols].rearrange("(h p) o -> p h o", p=P), y[:])

@@ -37,47 +37,51 @@ def tile_list_oneforboth_twoboards_one_tabled_kernel(
 
         def scale_plane(name, width, engine):
             tile = keep.tile([P, width], U8, name=name, align_bytes=64)
+            engine.memset(tile[:].bitcast(I32), 0)
             return tile
 
-        def load_scales(tile, src, queue):
+        def load_scale_rows(tile, src, q, queue):
+            queue.dma_start(tile[32 * q : 32 * q + 4, :].bitcast(I32), src[0, 4 * q : 4 * q + 4, :].bitcast(I32))
+
+        def load_scales(tile, src, queues):
             for q in range(4):
-                queue.dma_start(
-                    tile[32 * q : 32 * q + 32, :].bitcast(I32),
-                    src[0, 4 * q : 4 * q + 4, :].bitcast(I32).partition_broadcast(8),
-                )
+                load_scale_rows(tile, src, q, queues[q])
 
         xt_s = scale_plane("xt_s", T, nc.vector)
         w_s = scale_plane("w_s", R, nc.vector)
-        xo_s = scale_plane("xo_s", Z, nc.vector)
-        wb_s = scale_plane("wb_s", N, nc.vector)
+        xo_s = scale_plane("xo_s", Z, nc.gpsimd)
+        wb_s = scale_plane("wb_s", N, nc.gpsimd)
 
         l_xt = load_list("l_xt", offs)
         xt_w = keep.tile([P, T], U16, align_bytes=64)
-        nc.sync.dma_start(xt_w[:].bitcast(I32), xt_words[0].bitcast(I32))
+        nc.scalar.dma_start(xt_w[:].bitcast(I32), xt_words[0].bitcast(I32))
+        load_scales(xt_s, xt_scales, [nc.sync, nc.scalar, nc.sync, nc.scalar])
         w_w = keep.tile([P, R], I32, align_bytes=64)
-        nc.scalar.dma_start(w_w[:], w_words[0].rearrange("p n t -> p (n t)").bitcast(I32))
-        load_scales(xt_s, xt_scales, nc.sync)
-        load_scales(w_s, w_scales, nc.scalar)
-        l_pw_put = load_list("l_pw_put", offs3)
-        l_xo = load_list("l_xo", offs2)
+        nc.sync.dma_start(w_w[:], w_words[0].rearrange("p n t -> p (n t)").bitcast(I32))
         xo_w = keep.tile([P, Z], U32, align_bytes=64)
-        nc.sync.dma_start(xo_w[:].bitcast(I32), xo_words[0].rearrange("p n t -> p (n t)").bitcast(I32))
-        load_scales(xo_s, xo_scales, nc.sync)
+        nc.scalar.dma_start(xo_w[:].bitcast(I32), xo_words[0].rearrange("p n t -> p (n t)").bitcast(I32))
+        load_scales(w_s, w_scales, [nc.sync, nc.scalar, nc.sync, nc.scalar])
+        load_scale_rows(xo_s, xo_scales, 0, nc.sync)
+        l_xo = load_list("l_xo", offs2)
+        for q in range(1, 4):
+            load_scale_rows(xo_s, xo_scales, q, nc.sync)
+        l_pw_put = load_list("l_pw_put", offs3)
         l_pv_put = load_list("l_pv_put", offs4)
-        l_pw_get = load_list("l_pw_get", offs5)
-        l_pv_get = load_list("l_pv_get", offs6)
-        l_tz = load_list("l_tz", offs7)
         tz_sb = [keep.tile([P, E], F32, name="tz%d" % h) for h in range(2)]
         for h in range(2):
             nc.sync.dma_start(tz_sb[h][:], tz[h * P : (h + 1) * P, :])
+        l_pw_get = load_list("l_pw_get", offs5)
+        l_pv_get = load_list("l_pv_get", offs6)
+        l_tz = load_list("l_tz", offs7)
         wb_w = keep.tile([P, 2 * N], U8, align_bytes=64)
         nc.sync.dma_start(wb_w[:].bitcast(I32), wb_words[0].bitcast(I32))
-        load_scales(wb_s, wb_scales, nc.sync)
+        load_scales(wb_s, wb_scales, [nc.sync] * 4)
 
         pw = [keep.tile([P, C], F32, name="pw%d" % t) for t in range(PACK)]
         pv = [keep.tile([P, C], F32, name="pv%d" % t) for t in range(PACK)]
-        for board in pw + pv:
-            nc.vector.memset(board[:], 0.0)
+        for t in range(PACK):
+            nc.vector.memset(pw[t][:], 0.0)
+            nc.gpsimd.memset(pv[t][:], 0.0)
 
         xt_gw = keep.tile([P, J], U16, align_bytes=64)
         xt_gs = keep.tile([P, J], U8, align_bytes=64)
@@ -85,29 +89,33 @@ def tile_list_oneforboth_twoboards_one_tabled_kernel(
         nc.vector.tensor_copy(xt_gs[:], xt_s[:].indirect(l_xt[:]))
 
         wp_w = keep.tile([P, R], I32, align_bytes=64)
-        wp_s = keep.tile([P, R], U8, align_bytes=64)
+        wp_s = [keep.tile([P, 2 * P], U8, name="wp_s%d" % u, align_bytes=64) for u in range(2)]
         nc.vector.tensor_copy(
             wp_w[:].rearrange("p (t c i) -> p c t i", t=PACK, i=4),
             w_w[:].rearrange("p (c i t) -> p c t i", t=PACK, i=4),
         )
-        nc.vector.tensor_copy(
-            wp_s[:].rearrange("p (t c i) -> p c t i", t=PACK, i=16),
-            w_s[:].rearrange("p (c i t) -> p c t i", t=PACK, i=16),
-        )
+        for u in range(2):
+            nc.vector.tensor_copy(
+                wp_s[u][:].rearrange("p (t c i) -> p c t i", t=2, i=16),
+                w_s[:].rearrange("p (c i t) -> p c t i", t=PACK, i=16)[:, :, 2 * u : 2 * u + 2, :],
+            )
 
-        def first_stage(name, codes, scales):
-            banks = [psum.tile([P, 2, J], F32, name="%s_ps%d" % (name, u)) for u in range(2)]
-            for t in range(PACK):
-                cols = slice(t * P, (t + 1) * P)
-                nc.tensor.matmul_mx(
-                    out=banks[t // 2][:, t % 2, :],
-                    lhsT=wp_w[:, cols].bitcast(E4M3X4), lhsT_scale=wp_s[:, cols],
-                    rhs=codes, rhs_scale=scales, start=True, stop=True,
-                )
-            return banks
+        def first_stage(dst, t, codes, scales):
+            nc.tensor.matmul_mx(
+                out=dst,
+                lhsT=wp_w[:, t * P : (t + 1) * P].bitcast(E4M3X4),
+                lhsT_scale=wp_s[t // 2][:, (t % 2) * P : (t % 2 + 1) * P],
+                rhs=codes, rhs_scale=scales, start=True, stop=True,
+            )
 
-        a_ps = first_stage("a", xt_gw[:].bitcast(E2M1X4), xt_gs[:])
-        a_sb = [keep.tile([P, 2, J], F32, name="a_sb%d" % u) for u in range(2)]
+        a_ps0 = psum.tile([P, J], F32)
+        a_ps1 = psum.tile([P, J], F32)
+        a_ps23 = psum.tile([P, 2, J], F32)
+        for t, dst in enumerate([a_ps0[:], a_ps1[:], a_ps23[:, 0, :], a_ps23[:, 1, :]]):
+            first_stage(dst, t, xt_gw[:].bitcast(E2M1X4), xt_gs[:])
+        a_sb0 = keep.tile([P, J], F32)
+        a_sb1 = keep.tile([P, J], F32)
+        a_sb23 = keep.tile([P, 2, J], F32)
         b_sb = [keep.tile([P, 2, J], F32, name="b_sb%d" % u) for u in range(2)]
 
         def put(engine, board, lst, src):
@@ -122,21 +130,23 @@ def tile_list_oneforboth_twoboards_one_tabled_kernel(
             else:
                 nc.scalar.activation(dst, window[:].indirect(lst[:]), ACT.Copy)
 
-        nc.scalar.copy(a_sb[0][:], a_ps[0][:])
-        put("s", pw[0], l_pw_put, a_sb[0][:, 0, :])
-        put("v", pw[1], l_pw_put, a_sb[0][:, 1, :])
-        nc.scalar.copy(a_sb[1][:], a_ps[1][:])
-        put("s", pw[2], l_pw_put, a_sb[1][:, 0, :])
-        put("s", pw[3], l_pw_put, a_sb[1][:, 1, :])
-
         xo_gw = keep.tile([P, J], U32, align_bytes=64)
         xo_gs = keep.tile([P, J], U8, align_bytes=64)
         nc.vector.tensor_copy(xo_gw[:], xo_w[:].indirect(l_xo[:]))
         nc.vector.tensor_copy(xo_gs[:], xo_s[:].indirect(l_xo[:]))
-        b_ps = first_stage("b", xo_gw[:].bitcast(E4M3X4), xo_gs[:])
+        b_ps = [psum.tile([P, 2, J], F32, name="b_ps%d" % u) for u in range(2)]
+        for t in range(PACK):
+            first_stage(b_ps[t // 2][:, t % 2, :], t, xo_gw[:].bitcast(E4M3X4), xo_gs[:])
 
+        nc.scalar.copy(a_sb0[:], a_ps0[:])
+        put("s", pw[0], l_pw_put, a_sb0[:])
+        nc.vector.tensor_copy(a_sb1[:], a_ps1[:])
+        put("v", pw[1], l_pw_put, a_sb1[:])
+        nc.scalar.copy(a_sb23[:], a_ps23[:])
         nc.scalar.copy(b_sb[0][:], b_ps[0][:])
-        put("v", pv[0], l_pv_put, b_sb[0][:, 0, :])
+        put("s", pw[2], l_pw_put, a_sb23[:, 0, :])
+        put("v", pw[3], l_pw_put, a_sb23[:, 1, :])
+        put("s", pv[0], l_pv_put, b_sb[0][:, 0, :])
         put("v", pv[1], l_pv_put, b_sb[0][:, 1, :])
         nc.scalar.copy(b_sb[1][:], b_ps[1][:])
         put("s", pv[2], l_pv_put, b_sb[1][:, 0, :])

@@ -35,36 +35,23 @@ def tile_list_oneforboth_twoboards_one_tabled_kernel(
             nc.sync.dma_start(tile[:], src)
             return tile
 
-        def scale_plane(name, width, engine):
-            tile = keep.tile([P, width], U8, name=name, align_bytes=64)
-            engine.memset(tile[:].bitcast(I32), 0)
+        def load_scales(name, src, queue):
+            tile = keep.tile([P, src.shape[2]], U8, name=name, align_bytes=64)
+            queue.dma_start(tile[0:84, :].bitcast(I32), src[0, 0:14, :].bitcast(I32).partition_broadcast(6))
+            queue.dma_start(tile[84:128, :].bitcast(I32), src[0, 12:16, :].bitcast(I32).partition_broadcast(11))
             return tile
-
-        def load_scale_rows(tile, src, q, queue):
-            queue.dma_start(tile[32 * q : 32 * q + 4, :].bitcast(I32), src[0, 4 * q : 4 * q + 4, :].bitcast(I32))
-
-        def load_scales(tile, src, queues):
-            for q in range(4):
-                load_scale_rows(tile, src, q, queues[q])
-
-        xt_s = scale_plane("xt_s", T, nc.vector)
-        w_s = scale_plane("w_s", R, nc.vector)
-        xo_s = scale_plane("xo_s", Z, nc.gpsimd)
-        wb_s = scale_plane("wb_s", N, nc.gpsimd)
 
         l_xt = load_list("l_xt", offs)
         xt_w = keep.tile([P, T], U16, align_bytes=64)
         nc.scalar.dma_start(xt_w[:].bitcast(I32), xt_words[0].bitcast(I32))
-        load_scales(xt_s, xt_scales, [nc.sync, nc.scalar, nc.sync, nc.scalar])
         w_w = keep.tile([P, R], I32, align_bytes=64)
         nc.sync.dma_start(w_w[:], w_words[0].rearrange("p n t -> p (n t)").bitcast(I32))
+        xt_s = load_scales("xt_s", xt_scales, nc.sync)
+        w_s = load_scales("w_s", w_scales, nc.scalar)
         xo_w = keep.tile([P, Z], U32, align_bytes=64)
         nc.scalar.dma_start(xo_w[:].bitcast(I32), xo_words[0].rearrange("p n t -> p (n t)").bitcast(I32))
-        load_scales(w_s, w_scales, [nc.sync, nc.scalar, nc.sync, nc.scalar])
-        load_scale_rows(xo_s, xo_scales, 0, nc.sync)
         l_xo = load_list("l_xo", offs2)
-        for q in range(1, 4):
-            load_scale_rows(xo_s, xo_scales, q, nc.sync)
+        xo_s = load_scales("xo_s", xo_scales, nc.sync)
         l_pw_put = load_list("l_pw_put", offs3)
         l_pv_put = load_list("l_pv_put", offs4)
         tz_sb = [keep.tile([P, E], F32, name="tz%d" % h) for h in range(2)]
@@ -72,21 +59,19 @@ def tile_list_oneforboth_twoboards_one_tabled_kernel(
             nc.sync.dma_start(tz_sb[h][:], tz[h * P : (h + 1) * P, :])
         l_pw_get = load_list("l_pw_get", offs5)
         l_pv_get = load_list("l_pv_get", offs6)
-        l_tz = load_list("l_tz", offs7)
         wb_w = keep.tile([P, 2 * N], U8, align_bytes=64)
         nc.sync.dma_start(wb_w[:].bitcast(I32), wb_words[0].bitcast(I32))
-        load_scales(wb_s, wb_scales, [nc.sync] * 4)
+        l_tz = load_list("l_tz", offs7)
+        wb_s = load_scales("wb_s", wb_scales, nc.sync)
 
         pw = [keep.tile([P, C], F32, name="pw%d" % t) for t in range(PACK)]
         pv = [keep.tile([P, C], F32, name="pv%d" % t) for t in range(PACK)]
-        for t in range(PACK):
-            nc.vector.memset(pw[t][:], 0.0)
-            nc.gpsimd.memset(pv[t][:], 0.0)
+        for board in pw + pv:
+            nc.vector.memset(board[:], 0.0)
 
         xt_gw = keep.tile([P, J], U16, align_bytes=64)
         xt_gs = keep.tile([P, J], U8, align_bytes=64)
         nc.vector.tensor_copy(xt_gw[:], xt_w[:].indirect(l_xt[:]))
-        nc.vector.tensor_copy(xt_gs[:], xt_s[:].indirect(l_xt[:]))
 
         wp_w = keep.tile([P, R], I32, align_bytes=64)
         wp_s = [keep.tile([P, 2 * P], U8, name="wp_s%d" % u, align_bytes=64) for u in range(2)]
@@ -94,6 +79,7 @@ def tile_list_oneforboth_twoboards_one_tabled_kernel(
             wp_w[:].rearrange("p (t c i) -> p c t i", t=PACK, i=4),
             w_w[:].rearrange("p (c i t) -> p c t i", t=PACK, i=4),
         )
+        nc.vector.tensor_copy(xt_gs[:], xt_s[:].indirect(l_xt[:]))
         for u in range(2):
             nc.vector.tensor_copy(
                 wp_s[u][:].rearrange("p (t c i) -> p c t i", t=2, i=16),

@@ -28,6 +28,7 @@ def tile_list_oneforboth_twoboards_one_tabled_kernel(
     nc = tc.nc
     with ExitStack() as ctx:
         keep = ctx.enter_context(tc.tile_pool(name="keep", bufs=1))
+        shared = ctx.enter_context(tc.tile_pool(name="shared", bufs=1))
         psum = ctx.enter_context(tc.psum_pool(name="psum", bufs=1))
 
         def load_list(name, src):
@@ -35,23 +36,25 @@ def tile_list_oneforboth_twoboards_one_tabled_kernel(
             nc.sync.dma_start(tile[:], src)
             return tile
 
-        def load_scales(name, src, queue):
-            tile = keep.tile([P, src.shape[2]], U8, name=name, align_bytes=64)
-            queue.dma_start(tile[0:84, :].bitcast(I32), src[0, 0:14, :].bitcast(I32).partition_broadcast(6))
-            queue.dma_start(tile[84:128, :].bitcast(I32), src[0, 12:16, :].bitcast(I32).partition_broadcast(11))
-            return tile
+        def load_scales(tile, src, queue_low, queue_high):
+            queue_low.dma_start(tile[0:84, :].bitcast(I32), src[0, 0:14, :].bitcast(I32).partition_broadcast(6))
+            queue_high.dma_start(tile[84:128, :].bitcast(I32), src[0, 12:16, :].bitcast(I32).partition_broadcast(11))
 
+        xt_s = shared.tile([P, T], U8, align_bytes=64, offset=4 * C - T // 2)
+        w_s = shared.tile([P, R], U8, align_bytes=64, offset=3 * 4 * C - R // 2)
+        xo_s = keep.tile([P, Z], U8, align_bytes=64)
+        wb_s = keep.tile([P, N], U8, align_bytes=64)
         l_xt = load_list("l_xt", offs)
         xt_w = keep.tile([P, T], U16, align_bytes=64)
         nc.scalar.dma_start(xt_w[:].bitcast(I32), xt_words[0].bitcast(I32))
         w_w = keep.tile([P, R], I32, align_bytes=64)
         nc.sync.dma_start(w_w[:], w_words[0].rearrange("p n t -> p (n t)").bitcast(I32))
-        xt_s = load_scales("xt_s", xt_scales, nc.sync)
-        w_s = load_scales("w_s", w_scales, nc.scalar)
+        load_scales(xt_s, xt_scales, nc.sync, nc.sync)
+        load_scales(w_s, w_scales, nc.scalar, nc.scalar)
         xo_w = keep.tile([P, Z], U32, align_bytes=64)
         nc.scalar.dma_start(xo_w[:].bitcast(I32), xo_words[0].rearrange("p n t -> p (n t)").bitcast(I32))
         l_xo = load_list("l_xo", offs2)
-        xo_s = load_scales("xo_s", xo_scales, nc.sync)
+        load_scales(xo_s, xo_scales, nc.scalar, nc.sync)
         l_pw_put = load_list("l_pw_put", offs3)
         l_pv_put = load_list("l_pv_put", offs4)
         tz_sb = [keep.tile([P, E], F32, name="tz%d" % h) for h in range(2)]
@@ -62,11 +65,11 @@ def tile_list_oneforboth_twoboards_one_tabled_kernel(
         wb_w = keep.tile([P, 2 * N], U8, align_bytes=64)
         nc.sync.dma_start(wb_w[:].bitcast(I32), wb_words[0].bitcast(I32))
         l_tz = load_list("l_tz", offs7)
-        wb_s = load_scales("wb_s", wb_scales, nc.sync)
+        load_scales(wb_s, wb_scales, nc.sync, nc.sync)
 
         pw = [keep.tile([P, C], F32, name="pw%d" % t) for t in range(PACK)]
-        pv = [keep.tile([P, C], F32, name="pv%d" % t) for t in range(PACK)]
-        for board in pw + pv:
+        pv = [shared.tile([P, C], F32, name="pv%d" % t, align_bytes=64, offset=4 * C * t) for t in range(PACK)]
+        for board in pw:
             nc.vector.memset(board[:], 0.0)
 
         xt_gw = keep.tile([P, J], U16, align_bytes=64)
@@ -74,23 +77,24 @@ def tile_list_oneforboth_twoboards_one_tabled_kernel(
         nc.vector.tensor_copy(xt_gw[:], xt_w[:].indirect(l_xt[:]))
 
         wp_w = keep.tile([P, R], I32, align_bytes=64)
-        wp_s = [keep.tile([P, 2 * P], U8, name="wp_s%d" % u, align_bytes=64) for u in range(2)]
+        wp_s = keep.tile([P, R], U8, align_bytes=64)
         nc.vector.tensor_copy(
             wp_w[:].rearrange("p (t c i) -> p c t i", t=PACK, i=4),
             w_w[:].rearrange("p (c i t) -> p c t i", t=PACK, i=4),
         )
+        nc.vector.tensor_copy(
+            wp_s[:].rearrange("p (t c i) -> p c t i", t=PACK, i=16),
+            w_s[:].rearrange("p (c i t) -> p c t i", t=PACK, i=16),
+        )
         nc.vector.tensor_copy(xt_gs[:], xt_s[:].indirect(l_xt[:]))
-        for u in range(2):
-            nc.vector.tensor_copy(
-                wp_s[u][:].rearrange("p (t c i) -> p c t i", t=2, i=16),
-                w_s[:].rearrange("p (c i t) -> p c t i", t=PACK, i=16)[:, :, 2 * u : 2 * u + 2, :],
-            )
+        for board in pv:
+            nc.gpsimd.memset(board[:], 0.0)
 
         def first_stage(dst, t, codes, scales):
             nc.tensor.matmul_mx(
                 out=dst,
                 lhsT=wp_w[:, t * P : (t + 1) * P].bitcast(E4M3X4),
-                lhsT_scale=wp_s[t // 2][:, (t % 2) * P : (t % 2 + 1) * P],
+                lhsT_scale=wp_s[:, t * P : (t + 1) * P],
                 rhs=codes, rhs_scale=scales, start=True, stop=True,
             )
 
@@ -129,9 +133,9 @@ def tile_list_oneforboth_twoboards_one_tabled_kernel(
         nc.vector.tensor_copy(a_sb1[:], a_ps1[:])
         put("v", pw[1], l_pw_put, a_sb1[:])
         nc.scalar.copy(a_sb23[:], a_ps23[:])
-        nc.scalar.copy(b_sb[0][:], b_ps[0][:])
         put("s", pw[2], l_pw_put, a_sb23[:, 0, :])
         put("v", pw[3], l_pw_put, a_sb23[:, 1, :])
+        nc.scalar.copy(b_sb[0][:], b_ps[0][:])
         put("s", pv[0], l_pv_put, b_sb[0][:, 0, :])
         put("v", pv[1], l_pv_put, b_sb[0][:, 1, :])
         nc.scalar.copy(b_sb[1][:], b_ps[1][:])
@@ -170,14 +174,22 @@ def tile_list_oneforboth_twoboards_one_tabled_kernel(
                 out=hid_w[:, cols].bitcast(E5M2X4), scales=hid_s[:, cols],
                 in_=hid[:, cols, :].rearrange("p o t -> p (o t)"),
             )
-            p_ps = psum.tile([P, 2, HALF], F32, name="p_ps%d" % u)
             y = keep.tile([P, 2, HALF], F32, name="y%d" % u)
+            if u == 0:
+                p_both = psum.tile([P, 2, HALF], F32)
+                p_ps = [p_both[:, 0, :], p_both[:, 1, :]]
+            else:
+                p_ps = [psum.tile([P, HALF], F32, name="p_last%d" % h)[:] for h in range(2)]
             for h in range(2):
                 nc.tensor.matmul_mx(
-                    out=p_ps[:, h, :],
+                    out=p_ps[h],
                     lhsT=wb_w[:, 2 * P * h : 2 * P * (h + 1)].bitcast(E2M1X4), lhsT_scale=wb_s[:, P * h : P * (h + 1)],
                     rhs=hid_w[:, cols].bitcast(E5M2X4), rhs_scale=hid_s[:, cols], start=True, stop=True,
                 )
-            nc.vector.tensor_tensor(y[:], p_ps[:], tz_g[:, :, cols], ALU.add)
+            if u == 0:
+                nc.vector.tensor_tensor(y[:], p_both[:], tz_g[:, :, cols], ALU.add)
+            else:
+                for h in range(2):
+                    nc.vector.tensor_tensor(y[:, h, :], p_ps[h], tz_g[:, h, cols], ALU.add)
             queue = nc.sync if u == 0 else nc.scalar
             queue.dma_start(out[:, cols].rearrange("(h p) o -> p h o", p=P), y[:])

@@ -19,6 +19,15 @@ ALU = mybir.AluOpType
 
 P = 128
 PACK = 4
+LAST = PACK - 1
+HALF = O // 2
+LIST_HALF = HALF // 16
+BOARD_BYTES = 4 * C
+
+LOW_PERIOD, LOW_REPEATS = 14, 6
+LOW_PARTS = LOW_PERIOD * LOW_REPEATS
+HIGH_FIRST_ROW, HIGH_PERIOD = 12, 4
+HIGH_REPEATS = (P - LOW_PARTS) // HIGH_PERIOD
 
 
 def tile_list_oneforboth_twoboards_one_tabled_kernel(
@@ -37,13 +46,16 @@ def tile_list_oneforboth_twoboards_one_tabled_kernel(
             return tile
 
         def load_scales(tile, src, queue_low, queue_high):
-            queue_low.dma_start(tile[0:84, :].bitcast(I32), src[0, 0:14, :].bitcast(I32).partition_broadcast(6))
-            queue_high.dma_start(tile[84:128, :].bitcast(I32), src[0, 12:16, :].bitcast(I32).partition_broadcast(11))
+            low = src[0, 0:LOW_PERIOD, :].bitcast(I32).partition_broadcast(LOW_REPEATS)
+            high = src[0, HIGH_FIRST_ROW : HIGH_FIRST_ROW + HIGH_PERIOD, :].bitcast(I32).partition_broadcast(HIGH_REPEATS)
+            queue_low.dma_start(tile[0:LOW_PARTS, :].bitcast(I32), low)
+            queue_high.dma_start(tile[LOW_PARTS:P, :].bitcast(I32), high)
 
-        xt_s = shared.tile([P, T], U8, align_bytes=64, offset=4 * C - T // 2)
-        w_s = shared.tile([P, R], U8, align_bytes=64, offset=3 * 4 * C - R // 2)
+        xt_s = shared.tile([P, T], U8, align_bytes=64, offset=BOARD_BYTES - T // 2)
+        w_s = shared.tile([P, R], U8, align_bytes=64, offset=3 * BOARD_BYTES - R // 2)
         xo_s = keep.tile([P, Z], U8, align_bytes=64)
         wb_s = keep.tile([P, N], U8, align_bytes=64)
+
         l_xt = load_list("l_xt", offs)
         xt_w = keep.tile([P, T], U16, align_bytes=64)
         nc.scalar.dma_start(xt_w[:].bitcast(I32), xt_words[0].bitcast(I32))
@@ -57,10 +69,10 @@ def tile_list_oneforboth_twoboards_one_tabled_kernel(
         load_scales(xo_s, xo_scales, nc.scalar, nc.sync)
         l_pw_put = load_list("l_pw_put", offs3)
         l_pv_put = load_list("l_pv_put", offs4)
+        l_pw_get = load_list("l_pw_get", offs5)
         tz_sb = [keep.tile([P, E], F32, name="tz%d" % h) for h in range(2)]
         for h in range(2):
             nc.sync.dma_start(tz_sb[h][:], tz[h * P : (h + 1) * P, :])
-        l_pw_get = load_list("l_pw_get", offs5)
         l_pv_get = load_list("l_pv_get", offs6)
         wb_w = keep.tile([P, 2 * N], U8, align_bytes=64)
         nc.sync.dma_start(wb_w[:].bitcast(I32), wb_words[0].bitcast(I32))
@@ -68,14 +80,13 @@ def tile_list_oneforboth_twoboards_one_tabled_kernel(
         load_scales(wb_s, wb_scales, nc.sync, nc.sync)
 
         pw = [keep.tile([P, C], F32, name="pw%d" % t) for t in range(PACK)]
-        pv = [shared.tile([P, C], F32, name="pv%d" % t, align_bytes=64, offset=4 * C * t) for t in range(PACK)]
+        pv = [shared.tile([P, C], F32, name="pv%d" % t, align_bytes=64, offset=BOARD_BYTES * t) for t in range(PACK)]
         for board in pw:
             nc.vector.memset(board[:], 0.0)
 
         xt_gw = keep.tile([P, J], U16, align_bytes=64)
         xt_gs = keep.tile([P, J], U8, align_bytes=64)
         nc.vector.tensor_copy(xt_gw[:], xt_w[:].indirect(l_xt[:]))
-
         wp_w = keep.tile([P, R], I32, align_bytes=64)
         wp_s = keep.tile([P, R], U8, align_bytes=64)
         nc.vector.tensor_copy(
@@ -91,10 +102,9 @@ def tile_list_oneforboth_twoboards_one_tabled_kernel(
             nc.gpsimd.memset(board[:], 0.0)
 
         def first_stage(dst, t, codes, scales):
+            cols = slice(t * P, (t + 1) * P)
             nc.tensor.matmul_mx(
-                out=dst,
-                lhsT=wp_w[:, t * P : (t + 1) * P].bitcast(E4M3X4),
-                lhsT_scale=wp_s[:, t * P : (t + 1) * P],
+                out=dst, lhsT=wp_w[:, cols].bitcast(E4M3X4), lhsT_scale=wp_s[:, cols],
                 rhs=codes, rhs_scale=scales, start=True, stop=True,
             )
 
@@ -108,18 +118,6 @@ def tile_list_oneforboth_twoboards_one_tabled_kernel(
         a_sb23 = keep.tile([P, 2, J], F32)
         b_sb = [keep.tile([P, 2, J], F32, name="b_sb%d" % u) for u in range(2)]
 
-        def put(engine, board, lst, src):
-            if engine == "v":
-                nc.vector.tensor_copy(board[:].indirect(lst[:]), src)
-            else:
-                nc.scalar.activation(board[:].indirect(lst[:]), src, ACT.Copy)
-
-        def get(engine, dst, window, lst):
-            if engine == "v":
-                nc.vector.tensor_copy(dst, window[:].indirect(lst[:]))
-            else:
-                nc.scalar.activation(dst, window[:].indirect(lst[:]), ACT.Copy)
-
         xo_gw = keep.tile([P, J], U32, align_bytes=64)
         xo_gs = keep.tile([P, J], U8, align_bytes=64)
         nc.vector.tensor_copy(xo_gw[:], xo_w[:].indirect(l_xo[:]))
@@ -129,67 +127,70 @@ def tile_list_oneforboth_twoboards_one_tabled_kernel(
             first_stage(b_ps[t // 2][:, t % 2, :], t, xo_gw[:].bitcast(E4M3X4), xo_gs[:])
 
         nc.scalar.copy(a_sb0[:], a_ps0[:])
-        put("s", pw[0], l_pw_put, a_sb0[:])
+        nc.scalar.activation(pw[0][:].indirect(l_pw_put[:]), a_sb0[:], ACT.Copy)
         nc.vector.tensor_copy(a_sb1[:], a_ps1[:])
-        put("v", pw[1], l_pw_put, a_sb1[:])
+        nc.vector.tensor_copy(pw[1][:].indirect(l_pw_put[:]), a_sb1[:])
         nc.scalar.copy(a_sb23[:], a_ps23[:])
-        put("s", pw[2], l_pw_put, a_sb23[:, 0, :])
-        put("v", pw[3], l_pw_put, a_sb23[:, 1, :])
+        nc.scalar.activation(pw[2][:].indirect(l_pw_put[:]), a_sb23[:, 0, :], ACT.Copy)
+        nc.vector.tensor_copy(pw[3][:].indirect(l_pw_put[:]), a_sb23[:, 1, :])
         nc.scalar.copy(b_sb[0][:], b_ps[0][:])
-        put("s", pv[0], l_pv_put, b_sb[0][:, 0, :])
-        put("v", pv[1], l_pv_put, b_sb[0][:, 1, :])
+        nc.scalar.activation(pv[0][:].indirect(l_pv_put[:]), b_sb[0][:, 0, :], ACT.Copy)
+        nc.vector.tensor_copy(pv[1][:].indirect(l_pv_put[:]), b_sb[0][:, 1, :])
         nc.scalar.copy(b_sb[1][:], b_ps[1][:])
-        put("s", pv[2], l_pv_put, b_sb[1][:, 0, :])
-        put("s", pv[3], l_pv_put, b_sb[1][:, 1, :])
+        nc.scalar.activation(pv[2][:].indirect(l_pv_put[:]), b_sb[1][:, 0, :], ACT.Copy)
+        nc.scalar.activation(pv[3][:].indirect(l_pv_put[:]), b_sb[1][:, 1, :], ACT.Copy)
 
         pw_g = [keep.tile([P, O], F32, name="pw_g%d" % t) for t in range(PACK)]
         diff = keep.tile([P, PACK, O], F32)
         tz_g = keep.tile([P, 2, O], F32)
         for t in range(PACK):
-            get("v", pw_g[t][:], pw[t], l_pw_get)
-        for t in range(PACK - 1):
+            nc.vector.tensor_copy(pw_g[t][:], pw[t][:].indirect(l_pw_get[:]))
+        for t in range(LAST):
             nc.vector.tensor_tensor(diff[:, t, :], pv[t][:].indirect(l_pv_get[:]), pw_g[t][:], ALU.subtract)
-        get("s", tz_g[:, 0, :], tz_sb[0], l_tz)
-        HALF = O // 2
+        nc.scalar.activation(tz_g[:, 0, :], tz_sb[0][:].indirect(l_tz[:]), ACT.Copy)
         hid = keep.tile([P, O, PACK], BF16, align_bytes=64)
         hid_w = keep.tile([P, O], U32, align_bytes=64)
         hid_s = keep.tile([P, O], U8, align_bytes=64)
-        t = PACK - 1
-        for u in range(2):
-            cols = slice(u * HALF, (u + 1) * HALF)
-            nc.vector.tensor_tensor(
-                diff[:, t, cols], pv[t][:].indirect(l_pv_get[:, u * 8 : (u + 1) * 8]), pw_g[t][:, cols], ALU.subtract
-            )
-        get("v", tz_g[:, 1, :], tz_sb[1], l_tz)
-        for u in range(2):
-            cols = slice(u * HALF, (u + 1) * HALF)
+        halves = [slice(u * HALF, (u + 1) * HALF) for u in range(2)]
+        for u, cols in enumerate(halves):
+            entries = l_pv_get[:, u * LIST_HALF : (u + 1) * LIST_HALF]
+            nc.vector.tensor_tensor(diff[:, LAST, cols], pv[LAST][:].indirect(entries), pw_g[LAST][:, cols], ALU.subtract)
+        nc.vector.tensor_copy(tz_g[:, 1, :], tz_sb[1][:].indirect(l_tz[:]))
+
+        for cols in halves:
             nc.scalar.activation(
                 hid[:, cols, :].rearrange("p (c i) t -> p c t i", i=4),
                 diff[:, :, cols].rearrange("p t (c i) -> p c t i", i=4),
                 ACT.Abs,
             )
-        for u in range(2):
-            cols = slice(u * HALF, (u + 1) * HALF)
+
+        def second_stage(dst, h, cols):
+            nc.tensor.matmul_mx(
+                out=dst,
+                lhsT=wb_w[:, 2 * P * h : 2 * P * (h + 1)].bitcast(E2M1X4), lhsT_scale=wb_s[:, P * h : P * (h + 1)],
+                rhs=hid_w[:, cols].bitcast(E5M2X4), rhs_scale=hid_s[:, cols], start=True, stop=True,
+            )
+
+        def quantise(cols):
             nc.vector.quantize_mx(
                 out=hid_w[:, cols].bitcast(E5M2X4), scales=hid_s[:, cols],
                 in_=hid[:, cols, :].rearrange("p o t -> p (o t)"),
             )
-            y = keep.tile([P, 2, HALF], F32, name="y%d" % u)
-            if u == 0:
-                p_both = psum.tile([P, 2, HALF], F32)
-                p_ps = [p_both[:, 0, :], p_both[:, 1, :]]
-            else:
-                p_ps = [psum.tile([P, HALF], F32, name="p_last%d" % h)[:] for h in range(2)]
-            for h in range(2):
-                nc.tensor.matmul_mx(
-                    out=p_ps[h],
-                    lhsT=wb_w[:, 2 * P * h : 2 * P * (h + 1)].bitcast(E2M1X4), lhsT_scale=wb_s[:, P * h : P * (h + 1)],
-                    rhs=hid_w[:, cols].bitcast(E5M2X4), rhs_scale=hid_s[:, cols], start=True, stop=True,
-                )
-            if u == 0:
-                nc.vector.tensor_tensor(y[:], p_both[:], tz_g[:, :, cols], ALU.add)
-            else:
-                for h in range(2):
-                    nc.vector.tensor_tensor(y[:, h, :], p_ps[h], tz_g[:, h, cols], ALU.add)
-            queue = nc.sync if u == 0 else nc.scalar
-            queue.dma_start(out[:, cols].rearrange("(h p) o -> p h o", p=P), y[:])
+
+        first, second = halves
+        quantise(first)
+        y_first = keep.tile([P, 2, HALF], F32)
+        p_first = psum.tile([P, 2, HALF], F32)
+        for h in range(2):
+            second_stage(p_first[:, h, :], h, first)
+        nc.vector.tensor_tensor(y_first[:], p_first[:], tz_g[:, :, first], ALU.add)
+        nc.sync.dma_start(out[:, first].rearrange("(h p) o -> p h o", p=P), y_first[:])
+
+        quantise(second)
+        y_second = keep.tile([P, 2, HALF], F32)
+        p_second = [psum.tile([P, HALF], F32, name="p_second%d" % h) for h in range(2)]
+        for h in range(2):
+            second_stage(p_second[h][:], h, second)
+        for h in range(2):
+            nc.vector.tensor_tensor(y_second[:, h, :], p_second[h][:], tz_g[:, h, second], ALU.add)
+        nc.scalar.dma_start(out[:, second].rearrange("(h p) o -> p h o", p=P), y_second[:])

from contextlib import ExitStack

import concourse.mybir as mybir

K, T, Z, J, R, C, O, N, E = 512, 1024, 1024, 256, 512, 512, 256, 256, 1024
FLOPS = 2 * K * R * J * 2 + 2 * R * N * O

F32 = mybir.dt.float32
BF16 = mybir.dt.bfloat16
I32 = mybir.dt.int32
U32 = mybir.dt.uint32
U16 = mybir.dt.uint16
U8 = mybir.dt.uint8
E4M3X4 = mybir.dt.float8_e4m3fn_x4
E5M2X4 = mybir.dt.float8_e5m2_x4
E2M1X4 = mybir.dt.float4_e2m1fn_x4
ACT = mybir.ActivationFunctionType
ALU = mybir.AluOpType

P = 128
PACK = 4
LAST = PACK - 1
HALF = O // 2
LIST_HALF = HALF // 16
BOARD_BYTES = 4 * C

LOW_PERIOD, LOW_REPEATS = 14, 6
LOW_PARTS = LOW_PERIOD * LOW_REPEATS
HIGH_FIRST_ROW, HIGH_PERIOD = 12, 4
HIGH_REPEATS = (P - LOW_PARTS) // HIGH_PERIOD


def tile_list_oneforboth_twoboards_one_tabled_kernel(
    tc, xt_words, xt_scales, xo_words, xo_scales, w_words, w_scales, wb_words, wb_scales, tz,
    offs, offs2, offs3, offs4, offs5, offs6, offs7, out,
):
    nc = tc.nc
    with ExitStack() as ctx:
        keep = ctx.enter_context(tc.tile_pool(name="keep", bufs=1))
        shared = ctx.enter_context(tc.tile_pool(name="shared", bufs=1))
        psum = ctx.enter_context(tc.psum_pool(name="psum", bufs=1))

        def load_list(name, src):
            tile = keep.tile([P, src.shape[1]], U16, name=name)
            nc.sync.dma_start(tile[:], src)
            return tile

        def load_scales(tile, src, queue_low, queue_high):
            low = src[0, 0:LOW_PERIOD, :].bitcast(I32).partition_broadcast(LOW_REPEATS)
            high = src[0, HIGH_FIRST_ROW : HIGH_FIRST_ROW + HIGH_PERIOD, :].bitcast(I32).partition_broadcast(HIGH_REPEATS)
            queue_low.dma_start(tile[0:LOW_PARTS, :].bitcast(I32), low)
            queue_high.dma_start(tile[LOW_PARTS:P, :].bitcast(I32), high)

        xt_s = shared.tile([P, T], U8, align_bytes=64, offset=BOARD_BYTES - T // 2)
        w_s = shared.tile([P, R], U8, align_bytes=64, offset=3 * BOARD_BYTES - R // 2)
        xo_s = keep.tile([P, Z], U8, align_bytes=64)
        wb_s = keep.tile([P, N], U8, align_bytes=64)

        l_xt = load_list("l_xt", offs)
        xt_w = keep.tile([P, T], U16, align_bytes=64)
        nc.scalar.dma_start(xt_w[:].bitcast(I32), xt_words[0].bitcast(I32))
        w_w = keep.tile([P, R], I32, align_bytes=64)
        nc.sync.dma_start(w_w[:], w_words[0].rearrange("p n t -> p (n t)").bitcast(I32))
        load_scales(xt_s, xt_scales, nc.sync, nc.sync)
        load_scales(w_s, w_scales, nc.scalar, nc.scalar)
        xo_w = keep.tile([P, Z], U32, align_bytes=64)
        nc.scalar.dma_start(xo_w[:].bitcast(I32), xo_words[0].rearrange("p n t -> p (n t)").bitcast(I32))
        l_xo = load_list("l_xo", offs2)
        load_scales(xo_s, xo_scales, nc.scalar, nc.sync)
        l_pw_put = load_list("l_pw_put", offs3)
        l_pv_put = load_list("l_pv_put", offs4)
        l_pw_get = load_list("l_pw_get", offs5)
        tz_sb = [keep.tile([P, E], F32, name="tz%d" % h) for h in range(2)]
        for h in range(2):
            nc.sync.dma_start(tz_sb[h][:], tz[h * P : (h + 1) * P, :])
        l_pv_get = load_list("l_pv_get", offs6)
        wb_w = keep.tile([P, 2 * N], U8, align_bytes=64)
        nc.sync.dma_start(wb_w[:].bitcast(I32), wb_words[0].bitcast(I32))
        l_tz = load_list("l_tz", offs7)
        load_scales(wb_s, wb_scales, nc.sync, nc.sync)

        pw = [keep.tile([P, C], F32, name="pw%d" % t) for t in range(PACK)]
        pv = [shared.tile([P, C], F32, name="pv%d" % t, align_bytes=64, offset=BOARD_BYTES * t) for t in range(PACK)]
        for board in pw:
            nc.vector.memset(board[:], 0.0)

        xt_gw = keep.tile([P, J], U16, align_bytes=64)
        xt_gs = keep.tile([P, J], U8, align_bytes=64)
        nc.vector.tensor_copy(xt_gw[:], xt_w[:].indirect(l_xt[:]))
        wp_w = keep.tile([P, R], I32, align_bytes=64)
        wp_s = keep.tile([P, R], U8, align_bytes=64)
        nc.vector.tensor_copy(
            wp_w[:].rearrange("p (t c i) -> p c t i", t=PACK, i=4),
            w_w[:].rearrange("p (c i t) -> p c t i", t=PACK, i=4),
        )
        nc.vector.tensor_copy(
            wp_s[:].rearrange("p (t c i) -> p c t i", t=PACK, i=16),
            w_s[:].rearrange("p (c i t) -> p c t i", t=PACK, i=16),
        )
        nc.vector.tensor_copy(xt_gs[:], xt_s[:].indirect(l_xt[:]))
        for board in pv:
            nc.gpsimd.memset(board[:], 0.0)

        def first_stage(dst, t, codes, scales):
            cols = slice(t * P, (t + 1) * P)
            nc.tensor.matmul_mx(
                out=dst, lhsT=wp_w[:, cols].bitcast(E4M3X4), lhsT_scale=wp_s[:, cols],
                rhs=codes, rhs_scale=scales, start=True, stop=True,
            )

        a_ps0 = psum.tile([P, J], F32)
        a_ps1 = psum.tile([P, J], F32)
        a_ps23 = psum.tile([P, 2, J], F32)
        for t, dst in enumerate([a_ps0[:], a_ps1[:], a_ps23[:, 0, :], a_ps23[:, 1, :]]):
            first_stage(dst, t, xt_gw[:].bitcast(E2M1X4), xt_gs[:])
        a_sb0 = keep.tile([P, J], F32)
        a_sb1 = keep.tile([P, J], F32)
        a_sb23 = keep.tile([P, 2, J], F32)
        b_sb = [keep.tile([P, 2, J], F32, name="b_sb%d" % u) for u in range(2)]

        xo_gw = keep.tile([P, J], U32, align_bytes=64)
        xo_gs = keep.tile([P, J], U8, align_bytes=64)
        nc.vector.tensor_copy(xo_gw[:], xo_w[:].indirect(l_xo[:]))
        nc.vector.tensor_copy(xo_gs[:], xo_s[:].indirect(l_xo[:]))
        b_ps = [psum.tile([P, 2, J], F32, name="b_ps%d" % u) for u in range(2)]
        for t in range(PACK):
            first_stage(b_ps[t // 2][:, t % 2, :], t, xo_gw[:].bitcast(E4M3X4), xo_gs[:])

        nc.scalar.copy(a_sb0[:], a_ps0[:])
        nc.scalar.activation(pw[0][:].indirect(l_pw_put[:]), a_sb0[:], ACT.Copy)
        nc.vector.tensor_copy(a_sb1[:], a_ps1[:])
        nc.vector.tensor_copy(pw[1][:].indirect(l_pw_put[:]), a_sb1[:])
        nc.scalar.copy(a_sb23[:], a_ps23[:])
        nc.scalar.activation(pw[2][:].indirect(l_pw_put[:]), a_sb23[:, 0, :], ACT.Copy)
        nc.vector.tensor_copy(pw[3][:].indirect(l_pw_put[:]), a_sb23[:, 1, :])
        nc.scalar.copy(b_sb[0][:], b_ps[0][:])
        nc.scalar.activation(pv[0][:].indirect(l_pv_put[:]), b_sb[0][:, 0, :], ACT.Copy)
        nc.vector.tensor_copy(pv[1][:].indirect(l_pv_put[:]), b_sb[0][:, 1, :])
        nc.scalar.copy(b_sb[1][:], b_ps[1][:])
        nc.scalar.activation(pv[2][:].indirect(l_pv_put[:]), b_sb[1][:, 0, :], ACT.Copy)
        nc.scalar.activation(pv[3][:].indirect(l_pv_put[:]), b_sb[1][:, 1, :], ACT.Copy)

        pw_g = [keep.tile([P, O], F32, name="pw_g%d" % t) for t in range(PACK)]
        diff = keep.tile([P, PACK, O], F32)
        tz_g = keep.tile([P, 2, O], F32)
        for t in range(PACK):
            nc.vector.tensor_copy(pw_g[t][:], pw[t][:].indirect(l_pw_get[:]))
        for t in range(LAST):
            nc.vector.tensor_tensor(diff[:, t, :], pv[t][:].indirect(l_pv_get[:]), pw_g[t][:], ALU.subtract)
        nc.scalar.activation(tz_g[:, 0, :], tz_sb[0][:].indirect(l_tz[:]), ACT.Copy)
        hid = keep.tile([P, O, PACK], BF16, align_bytes=64)
        hid_w = keep.tile([P, O], U32, align_bytes=64)
        hid_s = keep.tile([P, O], U8, align_bytes=64)
        halves = [slice(u * HALF, (u + 1) * HALF) for u in range(2)]
        for u, cols in enumerate(halves):
            entries = l_pv_get[:, u * LIST_HALF : (u + 1) * LIST_HALF]
            nc.vector.tensor_tensor(diff[:, LAST, cols], pv[LAST][:].indirect(entries), pw_g[LAST][:, cols], ALU.subtract)
        nc.vector.tensor_copy(tz_g[:, 1, :], tz_sb[1][:].indirect(l_tz[:]))

        for cols in halves:
            nc.scalar.activation(
                hid[:, cols, :].rearrange("p (c i) t -> p c t i", i=4),
                diff[:, :, cols].rearrange("p t (c i) -> p c t i", i=4),
                ACT.Abs,
            )

        def second_stage(dst, h, cols):
            nc.tensor.matmul_mx(
                out=dst,
                lhsT=wb_w[:, 2 * P * h : 2 * P * (h + 1)].bitcast(E2M1X4), lhsT_scale=wb_s[:, P * h : P * (h + 1)],
                rhs=hid_w[:, cols].bitcast(E5M2X4), rhs_scale=hid_s[:, cols], start=True, stop=True,
            )

        def quantise(cols):
            nc.vector.quantize_mx(
                out=hid_w[:, cols].bitcast(E5M2X4), scales=hid_s[:, cols],
                in_=hid[:, cols, :].rearrange("p o t -> p (o t)"),
            )

        first, second = halves
        quantise(first)
        y_first = keep.tile([P, 2, HALF], F32)
        p_first = psum.tile([P, 2, HALF], F32)
        for h in range(2):
            second_stage(p_first[:, h, :], h, first)
        nc.vector.tensor_tensor(y_first[:], p_first[:], tz_g[:, :, first], ALU.add)
        nc.sync.dma_start(out[:, first].rearrange("(h p) o -> p h o", p=P), y_first[:])

        quantise(second)
        y_second = keep.tile([P, 2, HALF], F32)
        p_second = [psum.tile([P, HALF], F32, name="p_second%d" % h) for h in range(2)]
        for h in range(2):
            second_stage(p_second[h][:], h, second)
        for h in range(2):
            nc.vector.tensor_tensor(y_second[:, h, :], p_second[h][:], tz_g[:, h, second], ALU.add)
        nc.scalar.dma_start(out[:, second].rearrange("(h p) o -> p h o", p=P), y_second[:])
